import numpy as np
import ml_dtypes


def mxq(x, axis, fmt="e4m3"):
    dtype, down = {"e4m3": (ml_dtypes.float8_e4m3fn, 7), "e5m2": (ml_dtypes.float8_e5m2, 14)}[fmt]
    v = np.moveaxis(np.asarray(x, np.float32).astype(ml_dtypes.bfloat16).astype(np.float64), axis, -1)
    blocks = v.reshape(v.shape[:-1] + (-1, 32))
    amax = np.abs(blocks).max(-1, keepdims=True)
    byte = np.maximum(np.where(amax > 0, np.frexp(amax)[1] - 1 + 127, 0) - down, 1)
    scale = np.exp2(byte - 127.0)
    codes = (blocks / scale).astype(np.float32).astype(dtype).astype(np.float64)
    return np.moveaxis((codes * scale).reshape(v.shape), -1, axis)


WIDE = False


def mx_kscale(k):
    if not WIDE:
        return np.ones(k)
    levels = np.array([10, -10, 5, -5, 0])
    if k % 512:
        return np.exp2(np.random.permutation(np.resize(levels, k // 32))).repeat(32)
    a = np.empty((k // 512, 16))
    for p in range(k // 512):
        a[p, :8] = np.random.permutation(np.resize(levels, 8))
        for g in range(8):
            far = levels[np.abs(levels - a[p, g]) >= 10]
            a[p, g + 8] = far[np.random.randint(len(far))]
    return np.exp2(a.ravel()).repeat(32)


def f64(x):
    return np.asarray(x).astype(np.float64)


def striped(idx):
    return np.tile(np.asarray(idx).reshape(-1, 16).T, (8, 1)).astype(np.uint16)


def unstriped(offs):
    return offs[:16].T.reshape(-1).astype(np.int64)


def striped8(idx):
    return np.asarray(idx).reshape(8, -1, 16).transpose(0, 2, 1).reshape(128, -1).astype(np.uint16)


def unstriped8(offs):
    return offs.reshape(8, 16, -1).transpose(0, 2, 1).reshape(8, -1).astype(np.int64)


def pick8(x, idx, run):
    r = np.arange(len(x))
    return x[r[:, None], idx[r % (8 * run) // run]]


E2M1 = np.array([0.0, 0.5, 1.0, 1.5, 2.0, 3.0, 4.0, 6.0, -0.0, -0.5, -1.0, -1.5, -2.0, -3.0, -4.0, -6.0])


def pack_weight(w, fmt):
    k, n = w.shape
    w = f64(np.asarray(w, np.float32).astype(ml_dtypes.bfloat16)).reshape(k // 32, 32, n)
    amax = np.abs(w).max(1)
    if fmt == "e4m3":
        byte = np.frexp(amax)[1] - 1 + 127 - 7
    else:
        mant, ex = np.frexp(amax / 6.0)
        byte = np.where(mant > 0.5, ex, ex - 1) + 127
    byte = np.clip(np.where(amax > 0, byte, 1), 1, 254)
    scaled = (w * np.exp2(127.0 - byte)[:, None, :]).reshape(k, n).astype(np.float32)
    by_word = np.ascontiguousarray(scaled.reshape(k // 512, 128, 4, n).transpose(0, 1, 3, 2))
    if fmt == "e4m3":
        words = by_word.astype(ml_dtypes.float8_e4m3fn).view(np.uint8)
    else:
        c = by_word.astype(ml_dtypes.float4_e2m1fn).view(np.uint8) & 0xF
        words = (c[..., 0::2] | (c[..., 1::2] << 4)).reshape(k // 512, 128, 2 * n)
    return np.ascontiguousarray(words), np.ascontiguousarray(byte.astype(np.uint8).reshape(k // 512, 16, n))


def unpack_weight(words, scales, fmt):
    g, _, n = scales.shape
    words = np.ascontiguousarray(words).reshape(g, 128, n, -1)
    if fmt == "e4m3":
        vals = words.view(ml_dtypes.float8_e4m3fn).astype(np.float64)
    else:
        nib = np.empty((g, 128, n, 4), np.uint8)
        nib[..., 0::2] = words & 0xF
        nib[..., 1::2] = words >> 4
        vals = E2M1[nib]
    vals = vals * np.repeat(np.exp2(scales.astype(np.float64) - 127.0), 8, axis=1)[..., None]
    return vals.transpose(0, 1, 3, 2).reshape(g * 512, n)


def sigmoid(v):
    return 1.0 / (1.0 + np.exp(-v))


K, R, F, T, J, M = 512, 128, 512, 2048, 512, 256


def setup_inputs():
    n = np.random.standard_normal
    idx = np.random.permutation(T)[:J]
    idx2 = np.stack([np.random.permutation(J)[:M] for _ in range(8)])
    idx3 = np.stack([np.random.permutation(J)[:M] for _ in range(8)])
    fk = mx_kscale(K)
    ff = mx_kscale(F)
    tabp = pack_weight(n((K, T)) / fk[:, None], "e4m3")
    dtabp = pack_weight(n((K, T)) / fk[:, None], "e4m3")
    return {
        "tab_words": tabp[0],
        "tab_scales": tabp[1],
        "w1": (n((K, R)) * 1 / np.sqrt(K) * fk[:, None]).astype(np.float32),
        "gain": (np.random.uniform(0.5, 1.5, (R, 1))).astype(np.float32),
        "wo": (n((F, R)) * 1 / np.sqrt(F) * ff[:, None]).astype(np.float32),
        "dy": (n((F, M)) / ff[:, None]).astype(np.float32),
        "dtab_words": dtabp[0],
        "dtab_scales": dtabp[1],
        "og": (np.random.uniform(0.7, 2.0, (R, 1))).astype(np.float32),
        "base": (0.3 * n((R, J))).astype(np.float32),
        "offs": striped(idx),
        "offs2": striped8(idx2),
        "offs3": striped8(idx3),
    }


def reference(tab_words, tab_scales, w1, gain, wo, dy, dtab_words, dtab_scales, og, base, offs, offs2, offs3):
    idx = unstriped(offs)
    idx2 = unstriped8(offs2)
    idx3 = unstriped8(offs3)
    tabu = unpack_weight(tab_words, tab_scales, "e4m3")
    dtabu = unpack_weight(dtab_words, dtab_scales, "e4m3")
    w1q = mxq(f64(w1), 0, "e4m3")
    tabidxg = tabu[:, idx]
    a = w1q.T @ tabidxg
    dtabidxg = dtabu[:, idx]
    ta = w1q.T @ dtabidxg
    h1 = a * f64(gain)
    woq = mxq(f64(wo), 0, "e4m3")
    dyq = mxq(f64(dy), 0, "e4m3")
    c0 = woq.T @ dyq
    xh1 = ta * f64(gain)
    xe1 = pick8(xh1, idx3, 16) * sigmoid(pick8(h1, idx3, 16)) * (1.0 - sigmoid(pick8(h1, idx3, 16))) * c0
    xs1 = np.zeros((R, J))
    xs1[np.arange(R)[:, None], idx2[np.arange(R) % 128 // 16]] = xe1
    xe2 = (pick8(xh1, idx2, 16) * c0 * sigmoid(pick8(h1, idx3, 16)) + pick8(xh1, idx3, 16) * sigmoid(pick8(h1, idx3, 16)) * (1.0 - sigmoid(pick8(h1, idx3, 16))) * c0 * pick8(h1, idx2, 16)) * (1.0 - sigmoid(pick8(h1, idx3, 16))) + pick8(xh1, idx3, 16) * sigmoid(pick8(h1, idx3, 16)) * (1.0 - sigmoid(pick8(h1, idx3, 16))) * (-1.0) * c0 * pick8(h1, idx2, 16) * sigmoid(pick8(h1, idx3, 16))
    xs2 = np.zeros((R, J))
    xs2[np.arange(R)[:, None], idx3[np.arange(R) % 128 // 16]] = xe2
    xe3 = pick8(xh1, idx3, 16) * sigmoid(pick8(h1, idx3, 16)) * (1.0 - sigmoid(pick8(h1, idx3, 16))) * c0 * (-1.0)
    xs3 = np.zeros((R, J))
    xs3[np.arange(R)[:, None], idx3[np.arange(R) % 128 // 16]] = xe3
    xdh1 = xs1 + xs2 + xs3
    xda = xdh1 * f64(gain)
    y = xda * f64(og) + f64(base)
    return y

@@ -1,0 +1,146 @@
+from contextlib import ExitStack
+
+import concourse.mybir as mybir
+
+F32 = mybir.dt.float32
+BF16 = mybir.dt.bfloat16
+I32 = mybir.dt.int32
+U32 = mybir.dt.uint32
+U16 = mybir.dt.uint16
+U8 = mybir.dt.uint8
+FP8X4 = mybir.dt.float8_e4m3fn_x4
+ALU = mybir.AluOpType
+ACT = mybir.ActivationFunctionType
+
+P = 128
+K, R, F, T, J, M = 512, 128, 512, 2048, 512, 256
+HALF = J // 2
+FLOPS = 2 * K * R * J * 2 + 2 * F * R * M
+
+
+def tile_attend_hvpairgates_kernel(tc, tab_words, tab_scales, w1, gain, wo, dy, dtab_words, dtab_scales, og, base, offs, offs2, offs3, out):
+    nc = tc.nc
+    with ExitStack() as ctx:
+        sb = ctx.enter_context(tc.tile_pool(name="sb", bufs=1))
+        ps = ctx.enter_context(tc.psum_pool(name="ps", bufs=1))
+
+        def tile(name, shape, dtype):
+            return sb.tile(shape, dtype, name=name, align_bytes=64)
+
+        lst = sb.tile([P, J // 16], U16, name="lst")
+        lst2 = sb.tile([P, M // 16], U16, name="lst2")
+        lst3 = sb.tile([P, M // 16], U16, name="lst3")
+        tw = tile("tw", [P, T], U32)
+        dw = tile("dw", [P, T], U32)
+        tsc = tile("tsc", [P, T], U8)
+        dsc = tile("dsc", [P, T], U8)
+        w1_raw = tile("w1_raw", [P, 4, R], F32)
+        wo_raw = tile("wo_raw", [P, 4, R], F32)
+        dy_raw = tile("dy_raw", [P, 4, M], F32)
+        base_sb = tile("base_sb", [P, J], F32)
+        gain_sb = tile("gain_sb", [P, 1], F32)
+        og_sb = tile("og_sb", [P, 1], F32)
+        win2 = tile("win2", [P, J], F32)
+        win3 = tile("win3", [P, J], F32)
+
+        def words(x):
+            return x[0].rearrange("p n t -> p (n t)").bitcast(I32)
+
+        def load_scales(eng, plane, scales, row0):
+            for q in range(4):
+                eng.dma_start(out=plane[32 * q + row0 : 32 * q + row0 + 4, :].bitcast(I32), in_=scales[0, 4 * q : 4 * q + 4, :].bitcast(I32))
+
+        nc.vector.memset(tsc[:].bitcast(I32), 0)
+        nc.vector.memset(dsc[:].bitcast(I32), 0)
+        nc.vector.memset(win2[:], 0.0)
+        nc.vector.memset(win3[:], 0.0)
+
+        warm = tile("warm", [P, 1], F32)
+        nc.vector.memset(warm[:], 0.0)
+        warm2 = tile("warm2", [P, 1], F32)
+        nc.scalar.activation(warm2[:], warm[:], ACT.Sigmoid)
+        nc.sync.dma_start(lst[:], offs)
+        nc.sync.dma_start(out=w1_raw[:], in_=w1.rearrange("(p t) r -> p t r", t=4))
+        load_scales(nc.sync, tsc, tab_scales, 0)
+        nc.sync.dma_start(out=tw[:].bitcast(I32), in_=words(tab_words))
+        nc.sync.dma_start(out=gain_sb[:], in_=gain)
+        nc.sync.dma_start(lst3[:], offs3)
+        load_scales(nc.sync, dsc, dtab_scales, 4)
+        nc.sync.dma_start(out=dw[:].bitcast(I32), in_=words(dtab_words))
+        nc.sync.dma_start(lst2[:], offs2)
+        nc.sync.dma_start(out=wo_raw[:], in_=wo.rearrange("(p t) r -> p t r", t=4))
+        nc.sync.dma_start(out=dy_raw[:], in_=dy.rearrange("(p t) m -> p t m", t=4))
+        nc.sync.dma_start(out=base_sb[:], in_=base)
+        nc.sync.dma_start(out=og_sb[:], in_=og)
+
+        g = tile("g", [P, 1], F32)
+        nc.vector.tensor_scalar(g[:], gain_sb[:], og_sb[:], -0.25, ALU.mult, ALU.mult)
+
+        def cast(name, raw, width):
+            grouped = tile(name + "_bf", [P, width, 4], BF16)
+            nc.scalar.copy(out=grouped[:], in_=raw[:].rearrange("p t w -> p w t"))
+            return grouped
+
+        def quantise(name, grouped, width):
+            codes = tile(name + "_codes", [P, width], U32)
+            scales = tile(name + "_scales", [P, width], U8)
+            nc.vector.quantize_mx(out=codes[:].bitcast(FP8X4), scales=scales[:], in_=grouped[:].rearrange("p w t -> p (w t)"))
+            return codes, scales
+
+        def gather_scales(name, plane):
+            picked = tile(name, [P, J], U8)
+            nc.vector.tensor_copy(picked[:], plane[:].indirect(lst[:]))
+            return picked
+
+        def first_layer(name, table, picked_scales, row0):
+            res = tile(name, [P, J], F32)
+            for h in range(2):
+                cols = slice(h * HALF, (h + 1) * HALF)
+                picked = tile(name + "_words%d" % h, [P, HALF], U32)
+                nc.vector.tensor_copy(picked[:], table[:].indirect(lst[:, h * HALF // 16 : (h + 1) * HALF // 16]))
+                acc = ps.tile([P, HALF], F32, name=name + "_acc%d" % h)
+                nc.tensor.matmul_mx(out=acc[:], lhsT=w1_codes[:].bitcast(FP8X4), lhsT_scale=w1_scales[:],
+                                    rhs=picked[:].bitcast(FP8X4), rhs_scale=picked_scales[row0:P, cols], start=True, stop=True)
+                nc.scalar.activation(res[:, cols], acc[:], ACT.Copy, scale=gain_sb[:])
+            return res
+
+        w1_bf = cast("w1", w1_raw, R)
+        tsp = gather_scales("tsp", tsc)
+        w1_codes, w1_scales = quantise("w1", w1_bf, R)
+        h1 = first_layer("h1", tw, tsp, 0)
+        s = tile("s", [P, M], F32)
+        nc.scalar.activation(s[:], h1[:].indirect(lst3[:]), ACT.Sigmoid)
+        w = tile("w", [P, M], F32)
+        nc.scalar.activation(w[:], s[:], ACT.Identity, bias=1.0, scale=-2.0)
+        dsp = gather_scales("dsp", dsc)
+        xh1 = first_layer("xh1", dw, dsp, 4)
+        sq = tile("sq", [P, M], F32)
+        nc.scalar.activation(sq[:], s[:], ACT.Square, bias=1.0, scale=-2.0)
+
+        wo_bf = cast("wo", wo_raw, R)
+        dy_bf = cast("dy", dy_raw, M)
+
+        v = tile("v", [P, M], F32)
+        nc.vector.tensor_tensor(v[:], h1[:].indirect(lst2[:]), w[:], ALU.mult)
+        x3 = tile("x3", [P, M], F32)
+        nc.vector.tensor_copy(x3[:], xh1[:].indirect(lst3[:]))
+        wo_codes, wo_scales = quantise("wo", wo_bf, R)
+        dy_codes, dy_scales = quantise("dy", dy_bf, M)
+        c0 = ps.tile([P, M], F32, name="c0")
+        nc.tensor.matmul_mx(out=c0[:], lhsT=wo_codes[:].bitcast(FP8X4), lhsT_scale=wo_scales[:],
+                            rhs=dy_codes[:].bitcast(FP8X4), rhs_scale=dy_scales[:], start=True, stop=True)
+        r = tile("r", [P, M], F32)
+        nc.vector.scalar_tensor_tensor(r[:], v[:], 1.0, x3[:], ALU.subtract, ALU.mult)
+        r2 = sb.tile([P, M], F32, name="r2", tag="dy_bf", align_bytes=64)
+        nc.vector.tensor_tensor(r2[:], xh1[:].indirect(lst2[:]), r[:], ALU.add)
+        cd = tile("cd", [P, M], F32)
+        nc.vector.scalar_tensor_tensor(cd[:], sq[:], 1.0, c0[:], ALU.subtract, ALU.mult)
+        nc.vector.tensor_tensor(win2[:].indirect(lst2[:]), x3[:], cd[:], ALU.mult)
+        nc.vector.tensor_tensor(win3[:].indirect(lst3[:]), r2[:], cd[:], ALU.mult)
+        part = tile("part", [P, J], F32)
+        nc.vector.scalar_tensor_tensor(part[:], win2[:], g[:], base_sb[:], ALU.mult, ALU.add)
+        for h in range(2):
+            cols = slice(h * HALF, (h + 1) * HALF)
+            res = tile("res%d" % h, [P, HALF], F32)
+            nc.vector.scalar_tensor_tensor(res[:], win3[:, cols], g[:], part[:, cols], ALU.mult, ALU.add)
+            (nc.sync, nc.scalar)[h].dma_start(out=out[:, cols], in_=res[:])

@@ -47,8 +47,8 @@ def tile_attend_hvpairgates_kernel(tc, tab_words, tab_scales, w1, gain, wo, dy, 
             return x[0].rearrange("p n t -> p (n t)").bitcast(I32)
 
         def load_scales(eng, plane, scales, row0):
-            for q in range(4):
-                eng.dma_start(out=plane[32 * q + row0 : 32 * q + row0 + 4, :].bitcast(I32), in_=scales[0, 4 * q : 4 * q + 4, :].bitcast(I32))
+            for i in range(4):
+                eng.dma_start(out=plane[row0 + i : P : 32, :].bitcast(I32), in_=scales[0, i:16:4, :].bitcast(I32))
 
         nc.vector.memset(tsc[:].bitcast(I32), 0)
         nc.vector.memset(dsc[:].bitcast(I32), 0)
@@ -71,10 +71,10 @@ def tile_attend_hvpairgates_kernel(tc, tab_words, tab_scales, w1, gain, wo, dy, 
         nc.sync.dma_start(out=wo_raw[:], in_=wo.rearrange("(p t) r -> p t r", t=4))
         nc.sync.dma_start(out=dy_raw[:], in_=dy.rearrange("(p t) m -> p t m", t=4))
         nc.sync.dma_start(out=base_sb[:], in_=base)
-        nc.sync.dma_start(out=og_sb[:], in_=og)
+        nc.gpsimd.dma_start(out=og_sb[:], in_=og)
 
         g = tile("g", [P, 1], F32)
-        nc.vector.tensor_scalar(g[:], gain_sb[:], og_sb[:], -0.25, ALU.mult, ALU.mult)
+        nc.gpsimd.tensor_scalar(g[:], gain_sb[:], og_sb[:], -0.25, ALU.mult, ALU.mult)
 
         def cast(name, raw, width):
             grouped = tile(name + "_bf", [P, width, 4], BF16)
@@ -131,14 +131,16 @@ def tile_attend_hvpairgates_kernel(tc, tab_words, tab_scales, w1, gain, wo, dy, 
                             rhs=dy_codes[:].bitcast(FP8X4), rhs_scale=dy_scales[:], start=True, stop=True)
         r = tile("r", [P, M], F32)
         nc.vector.scalar_tensor_tensor(r[:], v[:], 1.0, x3[:], ALU.subtract, ALU.mult)
-        r2 = sb.tile([P, M], F32, name="r2", tag="dy_bf", align_bytes=64)
+        r2 = sb.tile([P, M], F32, name="r2", tag="dy_raw", align_bytes=64)
         nc.vector.tensor_tensor(r2[:], xh1[:].indirect(lst2[:]), r[:], ALU.add)
         cd = tile("cd", [P, M], F32)
         nc.vector.scalar_tensor_tensor(cd[:], sq[:], 1.0, c0[:], ALU.subtract, ALU.mult)
         nc.vector.tensor_tensor(win2[:].indirect(lst2[:]), x3[:], cd[:], ALU.mult)
         nc.vector.tensor_tensor(win3[:].indirect(lst3[:]), r2[:], cd[:], ALU.mult)
         part = tile("part", [P, J], F32)
-        nc.vector.scalar_tensor_tensor(part[:], win2[:], g[:], base_sb[:], ALU.mult, ALU.add)
+        for h in range(2):
+            cols = slice(h * HALF, (h + 1) * HALF)
+            nc.vector.scalar_tensor_tensor(part[:, cols], win2[:, cols], g[:], base_sb[:, cols], ALU.mult, ALU.add)
         for h in range(2):
             cols = slice(h * HALF, (h + 1) * HALF)
             res = tile("res%d" % h, [P, HALF], F32)

@@ -60,10 +60,10 @@ def tile_attend_hvpairgates_kernel(tc, tab_words, tab_scales, w1, gain, wo, dy, 
         warm2 = tile("warm2", [P, 1], F32)
         nc.scalar.activation(warm2[:], warm[:], ACT.Sigmoid)
         nc.sync.dma_start(lst[:], offs)
+        nc.sync.dma_start(out=gain_sb[:], in_=gain)
         nc.sync.dma_start(out=w1_raw[:], in_=w1.rearrange("(p t) r -> p t r", t=4))
         load_scales(nc.sync, tsc, tab_scales, 0)
         nc.sync.dma_start(out=tw[:].bitcast(I32), in_=words(tab_words))
-        nc.sync.dma_start(out=gain_sb[:], in_=gain)
         nc.sync.dma_start(lst3[:], offs3)
         load_scales(nc.sync, dsc, dtab_scales, 4)
         nc.sync.dma_start(out=dw[:].bitcast(I32), in_=words(dtab_words))
@@ -71,14 +71,14 @@ def tile_attend_hvpairgates_kernel(tc, tab_words, tab_scales, w1, gain, wo, dy, 
         nc.sync.dma_start(out=wo_raw[:], in_=wo.rearrange("(p t) r -> p t r", t=4))
         nc.sync.dma_start(out=dy_raw[:], in_=dy.rearrange("(p t) m -> p t m", t=4))
         nc.sync.dma_start(out=base_sb[:], in_=base)
-        nc.gpsimd.dma_start(out=og_sb[:], in_=og)
+        nc.sync.dma_start(out=og_sb[:], in_=og)
 
         g = tile("g", [P, 1], F32)
         nc.gpsimd.tensor_scalar(g[:], gain_sb[:], og_sb[:], -0.25, ALU.mult, ALU.mult)
 
         def cast(name, raw, width):
             grouped = tile(name + "_bf", [P, width, 4], BF16)
-            nc.scalar.copy(out=grouped[:], in_=raw[:].rearrange("p t w -> p w t"))
+            nc.scalar.copy(out=grouped[:].rearrange("p (c i) t -> p c t i", i=4), in_=raw[:].rearrange("p t (c i) -> p c t i", i=4))
             return grouped
 
         def quantise(name, grouped, width):

@@ -55,10 +55,10 @@ def tile_attend_hvpairgates_kernel(tc, tab_words, tab_scales, w1, gain, wo, dy, 
         nc.vector.memset(win2[:], 0.0)
         nc.vector.memset(win3[:], 0.0)
 
-        warm = tile("warm", [P, 1], F32)
-        nc.vector.memset(warm[:], 0.0)
-        warm2 = tile("warm2", [P, 1], F32)
-        nc.scalar.activation(warm2[:], warm[:], ACT.Sigmoid)
+        zero = tile("zero", [P, 1], F32)
+        nc.vector.memset(zero[:], 0.0)
+        half = tile("half", [P, 1], F32)
+        nc.scalar.activation(half[:], zero[:], ACT.Sigmoid)
         nc.sync.dma_start(lst[:], offs)
         nc.sync.dma_start(out=gain_sb[:], in_=gain)
         nc.sync.dma_start(out=w1_raw[:], in_=w1.rearrange("(p t) r -> p t r", t=4))
@@ -73,8 +73,8 @@ def tile_attend_hvpairgates_kernel(tc, tab_words, tab_scales, w1, gain, wo, dy, 
         nc.sync.dma_start(out=base_sb[:], in_=base)
         nc.sync.dma_start(out=og_sb[:], in_=og)
 
-        g = tile("g", [P, 1], F32)
-        nc.gpsimd.tensor_scalar(g[:], gain_sb[:], og_sb[:], -0.25, ALU.mult, ALU.mult)
+        ngain = tile("ngain", [P, 1], F32)
+        nc.scalar.activation(ngain[:], gain_sb[:], ACT.Copy, scale=-1.0)
 
         def cast(name, raw, width):
             grouped = tile(name + "_bf", [P, width, 4], BF16)
@@ -114,8 +114,6 @@ def tile_attend_hvpairgates_kernel(tc, tab_words, tab_scales, w1, gain, wo, dy, 
         nc.scalar.activation(w[:], s[:], ACT.Identity, bias=1.0, scale=-2.0)
         dsp = gather_scales("dsp", dsc)
         xh1 = first_layer("xh1", dw, dsp, 4)
-        sq = tile("sq", [P, M], F32)
-        nc.scalar.activation(sq[:], s[:], ACT.Square, bias=1.0, scale=-2.0)
 
         wo_bf = cast("wo", wo_raw, R)
         dy_bf = cast("dy", dy_raw, M)
@@ -129,14 +127,21 @@ def tile_attend_hvpairgates_kernel(tc, tab_words, tab_scales, w1, gain, wo, dy, 
         c0 = ps.tile([P, M], F32, name="c0")
         nc.tensor.matmul_mx(out=c0[:], lhsT=wo_codes[:].bitcast(FP8X4), lhsT_scale=wo_scales[:],
                             rhs=dy_codes[:].bitcast(FP8X4), rhs_scale=dy_scales[:], start=True, stop=True)
+        sq = sb.tile([P, M], F32, name="sq", tag="dy_bf", align_bytes=64)
+        nc.scalar.activation(sq[:], s[:], ACT.Square, bias=half[:], scale=-1.0)
+        g = sb.tile([P, 1], F32, name="g", tag="s", align_bytes=64)
+        nc.scalar.activation(g[:], og_sb[:], ACT.Copy, scale=ngain[:])
         r = tile("r", [P, M], F32)
         nc.vector.scalar_tensor_tensor(r[:], v[:], 1.0, x3[:], ALU.subtract, ALU.mult)
         r2 = sb.tile([P, M], F32, name="r2", tag="dy_raw", align_bytes=64)
         nc.vector.tensor_tensor(r2[:], xh1[:].indirect(lst2[:]), r[:], ALU.add)
         cd = tile("cd", [P, M], F32)
-        nc.vector.scalar_tensor_tensor(cd[:], sq[:], 1.0, c0[:], ALU.subtract, ALU.mult)
+        for h in range(2):
+            picks = slice(h * P, (h + 1) * P)
+            nc.vector.scalar_tensor_tensor(cd[:, picks], sq[:, picks], 0.25, c0[:, picks], ALU.subtract, ALU.mult)
+        nc.vector.tensor_tensor(win3[:].indirect(lst3[:, 0:8]), r2[:, 0:P], cd[:, 0:P], ALU.mult)
         nc.vector.tensor_tensor(win2[:].indirect(lst2[:]), x3[:], cd[:], ALU.mult)
-        nc.vector.tensor_tensor(win3[:].indirect(lst3[:]), r2[:], cd[:], ALU.mult)
+        nc.vector.tensor_tensor(win3[:].indirect(lst3[:, 8:16]), r2[:, P:M], cd[:, P:M], ALU.mult)
         part = tile("part", [P, J], F32)
         for h in range(2):
             cols = slice(h * HALF, (h + 1) * HALF)

from contextlib import ExitStack

import concourse.mybir as mybir

F32 = mybir.dt.float32
BF16 = mybir.dt.bfloat16
I32 = mybir.dt.int32
U32 = mybir.dt.uint32
U16 = mybir.dt.uint16
U8 = mybir.dt.uint8
FP8X4 = mybir.dt.float8_e4m3fn_x4
ALU = mybir.AluOpType
ACT = mybir.ActivationFunctionType

P = 128
K, R, F, T, J, M = 512, 128, 512, 2048, 512, 256
HALF = J // 2
FLOPS = 2 * K * R * J * 2 + 2 * F * R * M


def tile_attend_hvpairgates_kernel(tc, tab_words, tab_scales, w1, gain, wo, dy, dtab_words, dtab_scales, og, base, offs, offs2, offs3, out):
    nc = tc.nc
    with ExitStack() as ctx:
        sb = ctx.enter_context(tc.tile_pool(name="sb", bufs=1))
        ps = ctx.enter_context(tc.psum_pool(name="ps", bufs=1))

        def tile(name, shape, dtype):
            return sb.tile(shape, dtype, name=name, align_bytes=64)

        lst = sb.tile([P, J // 16], U16, name="lst")
        lst2 = sb.tile([P, M // 16], U16, name="lst2")
        lst3 = sb.tile([P, M // 16], U16, name="lst3")
        tw = tile("tw", [P, T], U32)
        dw = tile("dw", [P, T], U32)
        tsc = tile("tsc", [P, T], U8)
        dsc = tile("dsc", [P, T], U8)
        w1_raw = tile("w1_raw", [P, 4, R], F32)
        wo_raw = tile("wo_raw", [P, 4, R], F32)
        dy_raw = tile("dy_raw", [P, 4, M], F32)
        base_sb = tile("base_sb", [P, J], F32)
        gain_sb = tile("gain_sb", [P, 1], F32)
        og_sb = tile("og_sb", [P, 1], F32)
        win2 = tile("win2", [P, J], F32)
        win3 = tile("win3", [P, J], F32)

        def words(x):
            return x[0].rearrange("p n t -> p (n t)").bitcast(I32)

        def load_scales(eng, plane, scales, row0):
            for i in range(4):
                eng.dma_start(out=plane[row0 + i : P : 32, :].bitcast(I32), in_=scales[0, i:16:4, :].bitcast(I32))

        nc.vector.memset(tsc[:].bitcast(I32), 0)
        nc.vector.memset(dsc[:].bitcast(I32), 0)
        nc.vector.memset(win2[:], 0.0)
        nc.vector.memset(win3[:], 0.0)

        zero = tile("zero", [P, 1], F32)
        nc.vector.memset(zero[:], 0.0)
        half = tile("half", [P, 1], F32)
        nc.scalar.activation(half[:], zero[:], ACT.Sigmoid)
        nc.sync.dma_start(lst[:], offs)
        nc.sync.dma_start(out=gain_sb[:], in_=gain)
        nc.sync.dma_start(out=w1_raw[:], in_=w1.rearrange("(p t) r -> p t r", t=4))
        load_scales(nc.sync, tsc, tab_scales, 0)
        nc.sync.dma_start(out=tw[:].bitcast(I32), in_=words(tab_words))
        nc.sync.dma_start(lst3[:], offs3)
        load_scales(nc.sync, dsc, dtab_scales, 4)
        nc.sync.dma_start(out=dw[:].bitcast(I32), in_=words(dtab_words))
        nc.sync.dma_start(lst2[:], offs2)
        nc.sync.dma_start(out=wo_raw[:], in_=wo.rearrange("(p t) r -> p t r", t=4))
        nc.sync.dma_start(out=dy_raw[:], in_=dy.rearrange("(p t) m -> p t m", t=4))
        nc.sync.dma_start(out=base_sb[:], in_=base)
        nc.sync.dma_start(out=og_sb[:], in_=og)

        ngain = tile("ngain", [P, 1], F32)
        nc.scalar.activation(ngain[:], gain_sb[:], ACT.Copy, scale=-1.0)

        def cast(name, raw, width):
            grouped = tile(name + "_bf", [P, width, 4], BF16)
            nc.scalar.copy(out=grouped[:].rearrange("p (c i) t -> p c t i", i=4), in_=raw[:].rearrange("p t (c i) -> p c t i", i=4))
            return grouped

        def quantise(name, grouped, width):
            codes = tile(name + "_codes", [P, width], U32)
            scales = tile(name + "_scales", [P, width], U8)
            nc.vector.quantize_mx(out=codes[:].bitcast(FP8X4), scales=scales[:], in_=grouped[:].rearrange("p w t -> p (w t)"))
            return codes, scales

        def gather_scales(name, plane):
            picked = tile(name, [P, J], U8)
            nc.vector.tensor_copy(picked[:], plane[:].indirect(lst[:]))
            return picked

        def first_layer(name, table, picked_scales, row0):
            res = tile(name, [P, J], F32)
            for h in range(2):
                cols = slice(h * HALF, (h + 1) * HALF)
                picked = tile(name + "_words%d" % h, [P, HALF], U32)
                nc.vector.tensor_copy(picked[:], table[:].indirect(lst[:, h * HALF // 16 : (h + 1) * HALF // 16]))
                acc = ps.tile([P, HALF], F32, name=name + "_acc%d" % h)
                nc.tensor.matmul_mx(out=acc[:], lhsT=w1_codes[:].bitcast(FP8X4), lhsT_scale=w1_scales[:],
                                    rhs=picked[:].bitcast(FP8X4), rhs_scale=picked_scales[row0:P, cols], start=True, stop=True)
                nc.scalar.activation(res[:, cols], acc[:], ACT.Copy, scale=gain_sb[:])
            return res

        w1_bf = cast("w1", w1_raw, R)
        tsp = gather_scales("tsp", tsc)
        w1_codes, w1_scales = quantise("w1", w1_bf, R)
        h1 = first_layer("h1", tw, tsp, 0)
        s = tile("s", [P, M], F32)
        nc.scalar.activation(s[:], h1[:].indirect(lst3[:]), ACT.Sigmoid)
        w = tile("w", [P, M], F32)
        nc.scalar.activation(w[:], s[:], ACT.Identity, bias=1.0, scale=-2.0)
        dsp = gather_scales("dsp", dsc)
        xh1 = first_layer("xh1", dw, dsp, 4)

        wo_bf = cast("wo", wo_raw, R)
        dy_bf = cast("dy", dy_raw, M)

        v = tile("v", [P, M], F32)
        nc.vector.tensor_tensor(v[:], h1[:].indirect(lst2[:]), w[:], ALU.mult)
        x3 = tile("x3", [P, M], F32)
        nc.vector.tensor_copy(x3[:], xh1[:].indirect(lst3[:]))
        wo_codes, wo_scales = quantise("wo", wo_bf, R)
        dy_codes, dy_scales = quantise("dy", dy_bf, M)
        c0 = ps.tile([P, M], F32, name="c0")
        nc.tensor.matmul_mx(out=c0[:], lhsT=wo_codes[:].bitcast(FP8X4), lhsT_scale=wo_scales[:],
                            rhs=dy_codes[:].bitcast(FP8X4), rhs_scale=dy_scales[:], start=True, stop=True)
        sq = sb.tile([P, M], F32, name="sq", tag="dy_bf", align_bytes=64)
        nc.scalar.activation(sq[:], s[:], ACT.Square, bias=half[:], scale=-1.0)
        g = sb.tile([P, 1], F32, name="g", tag="s", align_bytes=64)
        nc.scalar.activation(g[:], og_sb[:], ACT.Copy, scale=ngain[:])
        r = tile("r", [P, M], F32)
        nc.vector.scalar_tensor_tensor(r[:], v[:], 1.0, x3[:], ALU.subtract, ALU.mult)
        r2 = sb.tile([P, M], F32, name="r2", tag="dy_raw", align_bytes=64)
        nc.vector.tensor_tensor(r2[:], xh1[:].indirect(lst2[:]), r[:], ALU.add)
        cd = tile("cd", [P, M], F32)
        for h in range(2):
            picks = slice(h * P, (h + 1) * P)
            nc.vector.scalar_tensor_tensor(cd[:, picks], sq[:, picks], 0.25, c0[:, picks], ALU.subtract, ALU.mult)
        nc.vector.tensor_tensor(win3[:].indirect(lst3[:, 0:8]), r2[:, 0:P], cd[:, 0:P], ALU.mult)
        nc.vector.tensor_tensor(win2[:].indirect(lst2[:]), x3[:], cd[:], ALU.mult)
        nc.vector.tensor_tensor(win3[:].indirect(lst3[:, 8:16]), r2[:, P:M], cd[:, P:M], ALU.mult)
        part = tile("part", [P, J], F32)
        for h in range(2):
            cols = slice(h * HALF, (h + 1) * HALF)
            nc.vector.scalar_tensor_tensor(part[:, cols], win2[:, cols], g[:], base_sb[:, cols], ALU.mult, ALU.add)
        for h in range(2):
            cols = slice(h * HALF, (h + 1) * HALF)
            res = tile("res%d" % h, [P, HALF], F32)
            nc.vector.scalar_tensor_tensor(res[:], win3[:, cols], g[:], part[:, cols], ALU.mult, ALU.add)
            (nc.sync, nc.scalar)[h].dma_start(out=out[:, cols], in_=res[:])
